import numpy as np
import ml_dtypes


def mxq(x, axis, fmt="e4m3"):
    dtype, down = {"e4m3": (ml_dtypes.float8_e4m3fn, 7), "e5m2": (ml_dtypes.float8_e5m2, 14)}[fmt]
    v = np.moveaxis(np.asarray(x, np.float32).astype(ml_dtypes.bfloat16).astype(np.float64), axis, -1)
    blocks = v.reshape(v.shape[:-1] + (-1, 32))
    amax = np.abs(blocks).max(-1, keepdims=True)
    byte = np.maximum(np.where(amax > 0, np.frexp(amax)[1] - 1 + 127, 0) - down, 1)
    scale = np.exp2(byte - 127.0)
    codes = (blocks / scale).astype(np.float32).astype(dtype).astype(np.float64)
    return np.moveaxis((codes * scale).reshape(v.shape), -1, axis)


WIDE = False


def mx_kscale(k):
    if not WIDE:
        return np.ones(k)
    levels = np.array([10, -10, 5, -5, 0])
    if k % 512:
        return np.exp2(np.random.permutation(np.resize(levels, k // 32))).repeat(32)
    a = np.empty((k // 512, 16))
    for p in range(k // 512):
        a[p, :8] = np.random.permutation(np.resize(levels, 8))
        for g in range(8):
            far = levels[np.abs(levels - a[p, g]) >= 10]
            a[p, g + 8] = far[np.random.randint(len(far))]
    return np.exp2(a.ravel()).repeat(32)


BF16 = ml_dtypes.bfloat16


def bf(x):
    return np.asarray(x, np.float32).astype(BF16)


def f64(x):
    return np.asarray(x).astype(np.float64)


N, K, D = 1024, 1024, 1024


def draw0():
    t = mx_kscale(N)
    s = mx_kscale(K)
    return {"y": bf(np.random.standard_normal((N, K))),
            "w": bf(np.random.standard_normal((K, D)) * np.sqrt(N / K) / s[:, None]),
            "a": bf(np.random.uniform(0.5, 4.0, K)),
            "p": bf((1.0 + 0.1 * np.random.standard_normal(N)) * t),
            "u": bf((1.0 + 0.1 * np.random.standard_normal(N)) / t),
            "m": bf((1.0 + 0.1 * np.random.standard_normal(K)) * s)}


def sample_mean_outer(left_q, right_q):
    return (left_q.T @ right_q) / left_q.shape[0]


def core(y, w, a, p, u, m):
    y, w, a, p, u, m = f64(y), f64(w), f64(a), f64(p), f64(u), f64(m)
    phi = p[:, None] * np.tanh(a[None, :] * y)
    yl = p[:, None] * y
    yr = u[:, None] * y
    phi_q = mxq(phi, 0, "e4m3")
    yl_q = mxq(yl, 0, "e4m3")
    yr_q = mxq(yr, 0, "e4m3")
    r = sample_mean_outer(yl_q, yr_q)
    cm = sample_mean_outer(phi_q, yr_q)
    eye = np.eye(y.shape[1])
    g = r - eye + cm - cm.T
    gm = g * m[None, :]
    dw = -(mxq(gm, 1, "e4m3") @ mxq(w, 0, "e4m3"))
    return dw


def e4m3fn_bytes(y):
    return np.clip(np.asarray(y, np.float64), -448.0, 448.0).astype(np.float32).astype(ml_dtypes.float8_e4m3fn).view(np.uint8)


def e4m3fn_values(b):
    return np.asarray(b, np.uint8).view(ml_dtypes.float8_e4m3fn).astype(np.float64)


def setup_inputs():
    d = draw0()
    x0 = np.asarray(d['w']).astype(np.float64)
    s = (np.max(np.abs(x0), axis=(1,), keepdims=True) / 448.0).astype(np.float32)
    out = {}
    for k, v in d.items():
        if k == 'w':
            out['w_bytes'] = e4m3fn_bytes(x0 / s.astype(np.float64))
            out['w_scale'] = s
        else:
            out[k] = v
    return out


def reference(y, w_bytes, w_scale, a, p, u, m):
    return core(y, e4m3fn_values(w_bytes) * w_scale.astype(np.float64), a, p, u, m)

from contextlib import ExitStack

import concourse.mybir as mybir
from concourse.masks import make_identity

P = 128
DIM = 1024
FLOPS = 3 * 2 * DIM * DIM * DIM

F32 = mybir.dt.float32
BF16 = mybir.dt.bfloat16
U32 = mybir.dt.uint32
U8 = mybir.dt.uint8
FP8 = mybir.dt.float8_e4m3fn
FP8X4 = mybir.dt.float8_e4m3fn_x4
MULT = mybir.AluOpType.mult
SUB = mybir.AluOpType.subtract
TANH = mybir.ActivationFunctionType.Tanh
COPY = mybir.ActivationFunctionType.Copy


def tile_easirelativegradientupdate_kernel(tc, y, w_bytes, w_scale, a, p, u, m, out):
    nc = tc.nc
    with ExitStack() as ctx:
        keep = ctx.enter_context(tc.tile_pool(name="keep", bufs=1))
        stage = ctx.enter_context(tc.tile_pool(name="stage", bufs=2))
        psum = ctx.enter_context(tc.psum_pool(name="psum", bufs=1))
        ctx.enter_context(tc.manual_schedule())

        def small(src, spec, dtype, name, shape):
            t = keep.tile(shape, dtype, name=name)
            nc.scalar.dma_start(out=t[:], in_=src.rearrange(spec, p=P, t=4))
            return t

        y_v = y.rearrange("(g p t) (c i) -> g c p t i", p=P, t=4, c=2)
        y_sb = {}
        for c in range(2):
            for g in range(2):
                y_sb[g, c] = keep.tile([P, 4, 512], BF16, name="y_%d%d" % (g, c), align_bytes=64)
        nc.sync.dma_start(out=y_sb[0, 0][:], in_=y_v[0, 0])
        a_sb = small(a, "(c p t) -> p c t", BF16, "a_sb", [P, 2, 4])
        p_sb = small(p, "(c p t) -> p c t", BF16, "p_sb", [P, 2, 4])
        u_sb = small(u, "(c p t) -> p c t", BF16, "u_sb", [P, 2, 4])
        m_sb = small(m, "(c p t) -> p c t", BF16, "m_sb", [P, 2, 4])
        ws_sb = small(w_scale, "(c p t) o -> p c (t o)", F32, "ws_sb", [P, 2, 4])
        nc.sync.dma_start(out=y_sb[1, 0][:], in_=y_v[1, 0])
        nc.sync.dma_start(out=y_sb[0, 1][:], in_=y_v[0, 1])
        nc.sync.dma_start(out=y_sb[1, 1][:], in_=y_v[1, 1])
        w_v = w_bytes.rearrange("(c p t) d -> c p t d", p=P, t=4)
        wb = {}
        for c in range(2):
            wb[c] = keep.tile([P, 4, DIM], U8, name="wb_%d" % c, align_bytes=64)
            nc.sync.dma_start(out=wb[c][:], in_=w_v[c])

        warm = keep.tile([P, 1], F32, name="warm")
        nc.vector.memset(warm[:], 0.0)
        warm2 = keep.tile([P, 1], F32, name="warm2")
        nc.scalar.activation(out=warm2[:], in_=warm[:], func=TANH)
        ident = keep.tile([P, P], F32, name="ident")
        make_identity(nc, ident[:])
        ident_b = keep.tile([P, P], BF16, name="ident_b")
        nc.vector.tensor_copy(out=ident_b[:], in_=ident[:])
        a_f = keep.tile([P, 8], F32, name="a_f")
        nc.vector.tensor_copy(out=a_f[:], in_=a_sb[:].rearrange("p c t -> p (c t)"))
        m_f = keep.tile([P, 8], F32, name="m_f")
        m_diag = keep.tile([P, 8, P], BF16, name="m_diag")

        def late_constants():
            nc.vector.tensor_scalar(out=m_f[:], in0=m_sb[:].rearrange("p c t -> p (c t)"), scalar1=1.0 / DIM, scalar2=None, op0=MULT)
            nc.gpsimd.tensor_tensor(
                out=m_diag[:],
                in0=ident_b[:].unsqueeze(1).to_broadcast([P, 8, P]),
                in1=m_sb[:].rearrange("p c t -> p (c t)").unsqueeze(2).to_broadcast([P, 8, P]),
                op=MULT,
            )

        th = {}
        bank = {}
        ops = {}
        vecs = {"yl": p_sb, "yr": u_sb}

        def fwd(q, g):
            c, h = divmod(q, 2)
            words = y_sb[g, c][:].rearrange("p t i -> p (t i)").bitcast(F32)
            ps = psum.tile([P, 4, P], F32, name="in_ps", bufs=2)
            for t in range(4):
                nc.tensor.transpose(ps[:, t, :], words[:, 256 * t + h : 256 * (t + 1) : 2], ident[:])
            bank["fwd", q, g] = ps

        def tanh(q, g):
            halves = bank["fwd", q, g][:].rearrange("p t n -> p (t n)").bitcast(BF16)
            t = stage.tile([P, 2, 512], F32, name="th", bufs=6)
            for e in range(2):
                k = 2 * q + e
                nc.scalar.activation(out=t[:, e, :], in_=halves[:, e::2], func=TANH, scale=a_f[:, k : k + 1])
            th[q, g] = t

        def back(q, g, e):
            ps = psum.tile([P, 4, P], F32, name="back_ps", bufs=3)
            for t in range(4):
                nc.tensor.transpose(ps[:, t, :], th[q, g][:, e, P * t : P * (t + 1)], ident[:])
            bank["back", q, g, e] = ps

        def backs(q, part):
            for g, e in [(0, 0), (0, 1), (1, 0), (1, 1)][part]:
                back(q, g, e)

        def il_pe(q, g):
            c, h = divmod(q, 2)
            src = y_sb[g, c][:].rearrange("p t (m s) -> p s m t", s=4)
            ps = psum.tile([P, 2, P, 4], BF16, name="in_ps", bufs=2)
            for e in range(2):
                nc.tensor.matmul(ps[:, e], lhsT=ident_b[:], rhs=src[:, 2 * h + e], start=True, stop=True)
            bank["il", q, g] = ps

        yil = {}

        def il(q, g, eng="s"):
            c, h = divmod(q, 2)
            if q not in yil:
                yil[q] = stage.tile([P, 2, 2, P, 4], BF16, name="yil", bufs=2, align_bytes=64)
            src = y_sb[g, c][:].rearrange("p t (m s) -> p s m t", s=4)[:, 2 * h : 2 * h + 2]
            if eng == "s":
                nc.scalar.copy(out=yil[q][:, g], in_=src)
            else:
                nc.vector.tensor_copy(out=yil[q][:, g], in_=src)

        def gain(q, key, g=None):
            if (q, key) not in ops:
                ops[q, key] = stage.tile([P, 2, 256, 4], BF16, name=key + "_il", bufs=2, align_bytes=64)
            vec = vecs[key]
            if g is None:
                nc.vector.tensor_tensor(
                    out=ops[q, key][:], in0=yil[q][:].rearrange("p g e m t -> p g (e m) t"),
                    in1=vec[:].unsqueeze(2).to_broadcast([P, 2, 256, 4]), op=MULT)
            else:
                nc.vector.tensor_tensor(
                    out=ops[q, key][:, g], in0=bank["il", q, g][:].rearrange("p e m t -> p (e m) t"),
                    in1=vec[:, g, :].unsqueeze(1).to_broadcast([P, 256, 4]), op=MULT)

        def negate(q, eng="v"):
            ops[q, "yn"] = stage.tile([P, 2, 256, 4], BF16, name="yn_il", bufs=2, align_bytes=64)
            dst = ops[q, "yn"][:].rearrange("p g i t -> p (g i t)")
            src = ops[q, "yr"][:].rearrange("p g i t -> p (g i t)")
            if eng == "s":
                nc.scalar.activation(out=dst, in_=src, func=COPY, scale=-1.0)
            else:
                nc.vector.tensor_scalar(out=dst, in0=src, scalar1=-1.0, scalar2=None, op0=MULT)

        def phi(q, g, e):
            if (g, e) == (0, 0):
                ops[q, "phi"] = stage.tile([P, 2, 256, 4], BF16, name="phi_il", bufs=2, align_bytes=64)
            nc.vector.tensor_tensor(
                out=ops[q, "phi"][:, g, P * e : P * (e + 1), :],
                in0=bank["back", q, g, e][:].rearrange("p t n -> p n t"),
                in1=p_sb[:, g, :].unsqueeze(1).to_broadcast([P, P, 4]), op=MULT)

        codes = {}
        scales = {}

        def quant(dst, src_ap, width):
            codes[dst] = keep.tile([P, width], U32, name="cd_" + "_".join([str(x) for x in dst]), align_bytes=64)
            scales[dst] = keep.tile([P, width], U8, name="sc_" + "_".join([str(x) for x in dst]), align_bytes=64)
            nc.vector.quantize_mx(out=codes[dst][:].bitcast(FP8X4), scales=scales[dst][:], in_=src_ap)

        def q_op(q, key):
            quant((key, q), ops[q, key][:].rearrange("p g i t -> p (g i t)"), 512)

        def mx(o, l, lo, r, ro, n, start, stop):
            nc.tensor.matmul_mx(
                out=o,
                lhsT=codes[l][:, lo : lo + P].bitcast(FP8X4), lhsT_scale=scales[l][:, lo : lo + P],
                rhs=codes[r][:, ro : ro + n].bitcast(FP8X4), rhs_scale=scales[r][:, ro : ro + n],
                start=start, stop=stop)

        blocks = {}
        gm = {}
        rot = [0]
        RING = []

        def ring_tile(shape):
            tag, bufs = RING[rot[0] % len(RING)]
            rot[0] += 1
            return psum.tile(shape, F32, name=tag, bufs=bufs)

        def passes(jq, iq):
            r = ("yr", "yl")
            cm = ("yr", "phi")
            ct = ("phi", "yn")
            return [(k, g) for k in ((r, cm, ct) if jq > iq else (r, ct, cm)) for g in range(2)]

        def run_passes(jq, iq, e, part):
            every = passes(jq, iq)
            for n, ((l, r), g) in list(enumerate(every))[part]:
                mx(blocks[jq, iq][:, e], (l, jq), 256 * g + P * e, (r, iq), 256 * g, 256, n == 0, n == 5)

        def open_block(jq, iq):
            blocks[jq, iq] = ring_tile([P, 2, 256])
            run_passes(jq, iq, 0, slice(0, 4))

        def close_block(jq, iq):
            run_passes(jq, iq, 0, slice(4, 6))
            run_passes(jq, iq, 1, slice(0, 6))

        def block(jq, iq):
            open_block(jq, iq)
            close_block(jq, iq)

        def gm_tile(c, iq):
            if (c, iq) not in gm:
                gm[c, iq] = stage.tile([P, 4, 256], BF16, name="gm", bufs=8, align_bytes=64)
            return gm[c, iq]

        def block_out(jq, iq):
            c, h = divmod(jq, 2)
            dst = gm_tile(c, iq)
            ps = blocks[jq, iq]
            for e in range(2):
                k = 2 * jq + e
                t = 2 * h + e
                if jq != iq:
                    cols = slice(0, 256)
                else:
                    cols = slice(P * (1 - e), P * (2 - e))
                nc.scalar.activation(out=dst[:, t, cols], in_=ps[:, e, cols], func=COPY, scale=m_f[:, k : k + 1])

        def diag_out(q):
            c, h = divmod(q, 2)
            dst = gm_tile(c, q)
            ps = blocks[q, q]
            for e in range(2):
                k = 2 * q + e
                cols = slice(P * e, P * (e + 1))
                nc.vector.scalar_tensor_tensor(
                    out=dst[:, 2 * h + e, cols], in0=ps[:, e, cols], scalar=m_f[:, k : k + 1],
                    in1=m_diag[:, k, :], op0=MULT, op1=SUB)

        gi = {}

        def unit_il(c, iq):
            gi[c, iq] = stage.tile([P, 256, 4], BF16, name="gi", bufs=3, align_bytes=64)
            nc.vector.tensor_copy(out=gi[c, iq][:], in_=gm[c, iq][:].rearrange("p t i -> p i t"))

        def unit_q(c, iq):
            quant(("gm", c, iq), gi[c, iq][:].rearrange("p i t -> p (i t)"), 256)

        wp = {}
        wi = {}

        def widen(c, t):
            if t == 0:
                wp[c] = stage.tile([P, 4, DIM], BF16, name="wp", bufs=2, align_bytes=64)
            nc.scalar.activation(out=wp[c][:, t, :], in_=wb[c][:, t, :].bitcast(FP8), func=COPY, scale=ws_sb[:, c, t : t + 1])

        def w_il(c, d, eng="v"):
            wi[c, d] = stage.tile([P, 512, 4], BF16, name="wi", bufs=2, align_bytes=64)
            src = wp[c][:, :, 512 * d : 512 * (d + 1)].rearrange("p t i -> p i t")
            if eng == "s":
                nc.scalar.copy(out=wi[c, d][:], in_=src)
            else:
                nc.vector.tensor_copy(out=wi[c, d][:], in_=src)

        def w_q(c, d):
            quant(("w", c, d), wi[c, d][:].rearrange("p i t -> p (i t)"), 512)

        out_v = out.rearrange("(c m t) d -> c t m d", m=P, t=4)
        s2b = {}

        def s2(iq, e):
            for d in range(2):
                ps = ring_tile([P, 512])
                for c in range(2):
                    mx(ps[:], ("gm", c, iq), P * e, ("w", c, d), 0, 512, c == 0, c == 1)
                s2b[iq, e, d] = ps

        def s2_out(iq, e, engs, split=False):
            c, h = divmod(iq, 2)
            o = stage.tile([P, DIM], F32, name="o", bufs=8, align_bytes=64)
            dst = out_v[c, 2 * h + e]
            for d in range(2):
                cols = slice(512 * d, 512 * (d + 1))
                if engs[d] == "s":
                    nc.scalar.activation(out=o[:, cols], in_=s2b[iq, e, d][:], func=COPY, scale=-1.0)
                else:
                    nc.vector.tensor_scalar(out=o[:, cols], in0=s2b[iq, e, d][:], scalar1=-1.0, scalar2=None, op0=MULT)
                if split:
                    nc.sync.dma_start(out=dst[:, cols], in_=o[:, cols])
            if not split:
                nc.sync.dma_start(out=dst, in_=o[:])

        FIRST3 = slice(0, 3)
        LAST = slice(3, 4)

        RING.extend([("mx_ps", 3)])
        fwd(0, 0)
        tanh(0, 0)
        il_pe(0, 0)
        gain(0, "yr", 0)
        gain(0, "yl", 0)
        fwd(0, 1)
        tanh(0, 1)
        back(0, 0, 0)
        back(0, 0, 1)
        il_pe(0, 1)
        phi(0, 0, 0)
        gain(0, "yr", 1)
        gain(0, "yl", 1)
        phi(0, 0, 1)
        back(0, 1, 0)
        back(0, 1, 1)
        q_op(0, "yr")
        negate(0)
        q_op(0, "yl")
        phi(0, 1, 0)
        for g in range(2):
            fwd(1, g)
            il(1, g)
            tanh(1, g)
        phi(0, 1, 1)
        q_op(0, "yn")
        late_constants()
        q_op(0, "phi")
        backs(1, FIRST3)
        for g in range(2):
            fwd(2, g)
            tanh(2, g)

        def quarter(q, mids, neg="s"):
            gain(q, "yr")
            phi(q, 0, 0)
            if neg == "s":
                negate(q, "s")
            mids[0]()
            gain(q, "yl")
            phi(q, 0, 1)
            q_op(q, "yr")
            mids[1]()
            phi(q, 1, 0)
            if neg == "v":
                negate(q, "v")
            mids[2]()
            q_op(q, "yl")
            phi(q, 1, 1)
            q_op(q, "yn")
            mids[3]()
            q_op(q, "phi")

        def nothing():
            return None

        def m1a():
            block(0, 0)
            backs(1, LAST)
            il(2, 0)
            il(2, 1)
            block_out(0, 0)

        def m1b():
            fwd(3, 0)
            tanh(3, 0)
            fwd(3, 1)
            tanh(3, 1)

        quarter(1, [m1a, lambda: diag_out(0), m1b, nothing])
        backs(2, FIRST3)

        def m2a():
            il(3, 0)
            il(3, 1)
            block(1, 1)
            backs(2, LAST)
            block_out(1, 1)
            RING.extend([("in_ps", 2)] * 2)

        def m2b():
            diag_out(1)
            block(1, 0)
            block_out(1, 0)

        def m2c():
            block(0, 1)
            block_out(0, 1)
            widen(0, 0)

        quarter(2, [m2a, m2b, m2c, nothing])
        backs(3, FIRST3)

        def m3a():
            widen(0, 1)
            block(2, 2)
            backs(3, LAST)
            block_out(2, 2)
            widen(0, 2)
            block(2, 0)
            block_out(2, 0)
            widen(0, 3)

        def m3b():
            diag_out(2)
            block(2, 1)
            block_out(2, 1)
            widen(1, 0)

        def m3c():
            block(0, 2)
            block_out(0, 2)
            widen(1, 1)
            block(1, 2)
            block_out(1, 2)
            widen(1, 2)

        quarter(3, [m3a, m3b, m3c, nothing], "v")
        RING.extend([("back_ps", 3)] * 3)
        widen(1, 3)

        block(3, 3)
        block_out(3, 3)
        unit_il(0, 0)
        unit_il(0, 1)
        unit_q(0, 0)
        unit_q(0, 1)
        w_il(0, 0)
        diag_out(3)
        block(3, 0)
        block_out(3, 0)
        w_il(0, 1)
        w_q(0, 0)
        w_q(0, 1)
        w_il(1, 0)
        unit_il(1, 0)
        w_q(1, 0)
        w_il(1, 1)
        unit_q(1, 0)
        block(0, 3)
        block_out(0, 3)
        w_q(1, 1)
        block(1, 3)
        block_out(1, 3)
        block(2, 3)
        block_out(2, 3)
        unit_il(0, 3)
        block(3, 1)
        block_out(3, 1)
        s2(0, 0)
        unit_il(1, 3)
        s2_out(0, 0, "ss")
        unit_q(0, 3)
        unit_q(1, 3)
        s2(0, 1)
        unit_il(1, 1)
        s2_out(0, 1, "sv")
        unit_q(1, 1)
        block(3, 2)
        block_out(3, 2)
        s2(3, 0)
        unit_il(0, 2)
        s2_out(3, 0, "sv")
        unit_q(0, 2)
        s2(3, 1)
        unit_il(1, 2)
        s2_out(3, 1, "sv")
        unit_q(1, 2)
        for iq in (1, 2):
            for e in range(2):
                s2(iq, e)
                s2_out(iq, e, "sv", split=(iq, e) == (2, 1))
